import numpy as np
import ml_dtypes


def mxq(x, axis, fmt="e4m3"):
    dtype, down = {"e4m3": (ml_dtypes.float8_e4m3fn, 7), "e5m2": (ml_dtypes.float8_e5m2, 14)}[fmt]
    v = np.moveaxis(np.asarray(x, np.float32).astype(ml_dtypes.bfloat16).astype(np.float64), axis, -1)
    blocks = v.reshape(v.shape[:-1] + (-1, 32))
    amax = np.abs(blocks).max(-1, keepdims=True)
    byte = np.maximum(np.where(amax > 0, np.frexp(amax)[1] - 1 + 127, 0) - down, 1)
    scale = np.exp2(byte - 127.0)
    codes = (blocks / scale).astype(np.float32).astype(dtype).astype(np.float64)
    return np.moveaxis((codes * scale).reshape(v.shape), -1, axis)


WIDE = False


def mx_kscale(k):
    if not WIDE:
        return np.ones(k)
    levels = np.array([10, -10, 5, -5, 0])
    if k % 512:
        return np.exp2(np.random.permutation(np.resize(levels, k // 32))).repeat(32)
    a = np.empty((k // 512, 16))
    for p in range(k // 512):
        a[p, :8] = np.random.permutation(np.resize(levels, 8))
        for g in range(8):
            far = levels[np.abs(levels - a[p, g]) >= 10]
            a[p, g + 8] = far[np.random.randint(len(far))]
    return np.exp2(a.ravel()).repeat(32)


def f64(x):
    return np.asarray(x).astype(np.float64)


def striped(idx):
    return np.tile(idx.reshape(-1, 16).T, (8, 1)).astype(np.uint16)


def unstriped(offs):
    return offs[:16].T.reshape(-1).astype(np.int64)


def pack_weight(w):
    k, n = w.shape
    w = f64(np.asarray(w, np.float32).astype(ml_dtypes.bfloat16)).reshape(k // 32, 32, n)
    amax = np.abs(w).max(1)
    byte = np.clip(np.where(amax > 0, np.frexp(amax)[1] - 1 + 127 - 7, 1), 1, 254)
    scaled = (w * np.exp2(127.0 - byte)[:, None, :]).reshape(k, n).astype(np.float32)
    words = np.ascontiguousarray(scaled.reshape(k // 512, 128, 4, n).transpose(0, 1, 3, 2)).astype(ml_dtypes.float8_e4m3fn).view(np.uint8)
    return words, np.ascontiguousarray(byte.astype(np.uint8).reshape(k // 512, 16, n))


def unpack_weight(words, scales):
    g, p, n, _ = words.shape
    vals = np.ascontiguousarray(words).view(ml_dtypes.float8_e4m3fn).astype(np.float64) * np.repeat(np.exp2(scales.astype(np.float64) - 127.0), 8, axis=1)[..., None]
    return vals.transpose(0, 1, 3, 2).reshape(g * 512, n)


def sigmoid(v):
    return 1.0 / (1.0 + np.exp(-np.maximum(v, -700.0)))


K, T, S, V, N, H = 512, 2048, 512, 512, 512, 512


def setup_inputs():
    n = np.random.standard_normal
    s = mx_kscale(K)[:, None]
    u = mx_kscale(S)
    packed_xT = pack_weight(n((K, T)) * s)
    return {
        "x_words": packed_xT[0],
        "x_scales": packed_xT[1],
        "w1": (n((K, H)) / np.sqrt(K) / s).astype(np.float32),
        "gs": (np.random.uniform(0.5, 1.5, (K, 1)) / s).astype(np.float32),
        "gt": (np.random.uniform(0.5, 1.5, (V, 1)) * u[:, None]).astype(np.float32),
        "w2": (n((V, N)) / np.sqrt(V) / u[:, None]).astype(np.float32),
        "offs": striped(np.random.permutation(T)[:S]),
        "cand": striped(np.random.permutation(T)[:V]),
    }


def reference(x_words, x_scales, w1, gs, gt, w2, offs, cand):
    x_cand = unpack_weight(x_words, x_scales)[:, unstriped(cand)]
    xq = unpack_weight(x_words, x_scales)[:, unstriped(offs)]
    h = mxq(f64(w1), 0, "e4m3").T @ xq
    z = f64(gs) * h
    s = 0.0625 * ((x_cand.T @ mxq(z, 0, "e4m3")))
    z2 = f64(gt) * sigmoid(s)
    return mxq(f64(w2), 0, "e4m3").T @ mxq(z2, 0, "e4m3")

@@ -1,0 +1,187 @@
+from contextlib import ExitStack
+
+import concourse.mybir as mybir
+
+K, T, S, V, N, H = 512, 2048, 512, 512, 512, 512
+FLOPS = 2 * K * H * S + 2 * K * V * S + 2 * V * N * S
+
+F32 = mybir.dt.float32
+BF16 = mybir.dt.bfloat16
+I32 = mybir.dt.int32
+U32 = mybir.dt.uint32
+U16 = mybir.dt.uint16
+U8 = mybir.dt.uint8
+FP8X4 = mybir.dt.float8_e4m3fn_x4
+MULT = mybir.AluOpType.mult
+SIGMOID = mybir.ActivationFunctionType.Sigmoid
+
+P = 128
+PACK = 4
+CHUNK = 128
+CHUNKS = S // CHUNK
+HALF = 256
+
+
+def tile_picked_candread_sigmoid_p_kernel(
+    tc, x_words, x_scales, w1, gs, gt, w2, offs, cand, out
+):
+    nc = tc.nc
+    with ExitStack() as ctx:
+        keep = ctx.enter_context(tc.tile_pool(name="keep", bufs=1))
+        psum = ctx.enter_context(tc.psum_pool(name="psum", bufs=8))
+
+        offs_sb = keep.tile([P, S // 16], U16, name="offs_sb")
+        cand_sb = keep.tile([P, V // 16], U16, name="cand_sb")
+        table_words = keep.tile([P, T], U32, name="table_words", align_bytes=64)
+        table_scales = keep.tile([P, T], U8, name="table_scales", align_bytes=64)
+        gs_sb = keep.tile([P, PACK], F32, name="gs_sb")
+        gt_sb = keep.tile([P, PACK], F32, name="gt_sb")
+        warm = keep.tile([P, 2], F32, name="warm")
+
+        nc.vector.memset(table_scales[:].bitcast(I32), 0)
+        for q in range(4):
+            nc.scalar.dma_start(
+                out=table_scales[32 * q : 32 * q + 4, :].bitcast(I32),
+                in_=x_scales[0, 4 * q : 4 * q + 4, :].bitcast(I32),
+            )
+        nc.vector.memset(warm[:, 0:1], 0.0)
+        nc.scalar.activation(warm[:, 1:2], warm[:, 0:1], SIGMOID)
+
+        w1_raw = [keep.tile([P, PACK, HALF], F32, name="w1_raw%d" % i) for i in range(2)]
+        w2_raw = [keep.tile([P, PACK, HALF], F32, name="w2_raw%d" % i) for i in range(2)]
+        w1_rows = w1.rearrange("(p j) c -> p j c", j=PACK)
+        w2_rows = w2.rearrange("(p j) c -> p j c", j=PACK)
+        nc.sync.dma_start(out=w1_raw[0][:], in_=w1_rows[:, :, 0:HALF])
+        nc.sync.dma_start(offs_sb[:], offs)
+        nc.sync.dma_start(cand_sb[:], cand)
+        nc.sync.dma_start(out=w1_raw[1][:], in_=w1_rows[:, :, HALF:])
+        nc.sync.dma_start(
+            out=table_words[:].bitcast(I32),
+            in_=x_words[0].rearrange("p n t -> p (n t)").bitcast(I32),
+        )
+        for i in range(2):
+            nc.sync.dma_start(out=w2_raw[i][:], in_=w2_rows[:, :, i * HALF : (i + 1) * HALF])
+        nc.gpsimd.dma_start(out=gs_sb[:], in_=gs.rearrange("(p t) o -> p (t o)", t=PACK))
+        nc.gpsimd.dma_start(out=gt_sb[:], in_=gt.rearrange("(p t) o -> p (t o)", t=PACK))
+
+        tok_scales = keep.tile([P, S], U8, name="tok_scales", align_bytes=64)
+        cand_scales_listed = keep.tile([P, V], U8, name="cand_scales_listed", align_bytes=64)
+        cand_scales = keep.tile([P, V], U8, name="cand_scales", align_bytes=64)
+        nc.vector.tensor_copy(tok_scales[:], table_scales[:].indirect(offs_sb[:]))
+        nc.vector.tensor_copy(cand_scales_listed[:], table_scales[:].indirect(cand_sb[:]))
+        nc.vector.tensor_copy(
+            out=cand_scales[:].rearrange("p (t m) -> p m t", t=PACK),
+            in_=cand_scales_listed[:].rearrange("p (m t) -> p m t", t=PACK),
+        )
+
+        w1_bf = keep.tile([P, PACK, P, PACK], BF16, name="w1_bf", align_bytes=64)
+        for i in range(2):
+            nc.scalar.copy(
+                out=w1_bf[:, :, 64 * i : 64 * (i + 1), :].rearrange("p t m j -> p m j t"),
+                in_=w1_raw[i][:].rearrange("p j (m t) -> p m j t", t=PACK),
+            )
+        w1_words = keep.tile([P, H], U32, name="w1_words", align_bytes=64)
+        w1_scales = keep.tile([P, H], U8, name="w1_scales", align_bytes=64)
+        nc.vector.quantize_mx(
+            out=w1_words[:].bitcast(FP8X4),
+            scales=w1_scales[:],
+            in_=w1_bf[:].rearrange("p t m j -> p (t m j)"),
+        )
+
+        tok_words = [keep.tile([P, HALF], U32, name="tok_words%d" % i, align_bytes=64) for i in range(2)]
+        for i in range(2):
+            nc.vector.tensor_copy(tok_words[i][:], table_words[:].indirect(offs_sb[:, 16 * i : 16 * (i + 1)]))
+        cand_words = keep.tile([P, V], U32, name="cand_words", align_bytes=64)
+        nc.vector.tensor_copy(
+            cand_words[:].rearrange("p (t m) -> p m t", t=PACK), table_words[:].indirect(cand_sb[:])
+        )
+
+        w2_bf = keep.tile([P, N, PACK], BF16, name="w2_bf", align_bytes=64)
+        for i in range(2):
+            nc.scalar.copy(
+                out=w2_bf[:, HALF * i : HALF * (i + 1), :].rearrange("p (c e) j -> p c j e", e=4),
+                in_=w2_raw[i][:].rearrange("p j (c e) -> p c j e", e=4),
+            )
+
+        def product(words, scales, rhs_words, rhs_scales, first=0, count=PACK):
+            bank = psum.tile([P, count, CHUNK], F32, name="bank")
+            for t in range(first, first + count):
+                nc.tensor.matmul_mx(
+                    out=bank[:, t - first, :],
+                    lhsT=words[:, P * t : P * (t + 1)].bitcast(FP8X4),
+                    lhsT_scale=scales[:, P * t : P * (t + 1)],
+                    rhs=rhs_words.bitcast(FP8X4),
+                    rhs_scale=rhs_scales,
+                    start=True,
+                    stop=True,
+                )
+            return bank
+
+        def quantise(values, name):
+            words = keep.tile([P, CHUNK], U32, name=name + "_words", align_bytes=64)
+            scales = keep.tile([P, CHUNK], U8, name=name + "_scales", align_bytes=64)
+            nc.vector.quantize_mx(
+                out=words[:].bitcast(FP8X4), scales=scales[:], in_=values[:].rearrange("p n t -> p (n t)")
+            )
+            return words, scales
+
+        h_banks = []
+        for c in range(CHUNKS):
+            lo = (c % 2) * CHUNK
+            h_banks.append(
+                product(w1_words, w1_scales, tok_words[c // 2][:, lo : lo + CHUNK], tok_scales[:, c * CHUNK : (c + 1) * CHUNK])
+            )
+
+        z_bf = [keep.tile([P, CHUNK, PACK], BF16, name="z_bf%d" % c, align_bytes=64) for c in range(CHUNKS)]
+        sig = [keep.tile([P, CHUNK, PACK], F32, name="sig%d" % c) for c in range(CHUNKS)]
+        z2_bf = [keep.tile([P, CHUNK, PACK], BF16, name="z2_bf%d" % c, align_bytes=64) for c in range(CHUNKS)]
+        gs_wide = gs_sb[:].unsqueeze(1).to_broadcast([P, CHUNK, PACK])
+        gt_wide = gt_sb[:].unsqueeze(1).to_broadcast([P, CHUNK, PACK])
+
+        def weigh_features(c):
+            nc.vector.tensor_tensor(z_bf[c][:], h_banks[c][:].rearrange("p t n -> p n t"), gs_wide, MULT)
+
+        def score(c):
+            words, scales = quantise(z_bf[c], "z%d" % c)
+            bank = product(cand_words, cand_scales, words[:], scales[:])
+            nc.scalar.activation(sig[c][:], bank[:].rearrange("p t n -> p n t"), SIGMOID, scale=0.0625)
+
+        weigh_features(0)
+        for c in range(1, CHUNKS):
+            weigh_features(c)
+            score(c - 1)
+        w2_words = keep.tile([P, N], U32, name="w2_words", align_bytes=64)
+        w2_scales = keep.tile([P, N], U8, name="w2_scales", align_bytes=64)
+        nc.vector.quantize_mx(
+            out=w2_words[:].bitcast(FP8X4),
+            scales=w2_scales[:],
+            in_=w2_bf[:].rearrange("p m j -> p (m j)"),
+        )
+        score(CHUNKS - 1)
+
+        out_rows = out.rearrange("(b p) n -> p b n", p=P)
+
+        def weigh_candidates(c):
+            nc.vector.tensor_tensor(z2_bf[c][:], sig[c][:], gt_wide, MULT)
+
+        def read_out(c):
+            words, scales = quantise(z2_bf[c], "y%d" % c)
+            bank = product(w2_words, w2_scales, words[:], scales[:])
+            res = keep.tile([P, PACK, CHUNK], F32, name="res%d" % c)
+            nc.scalar.copy(out=res[:], in_=bank[:])
+            nc.sync.dma_start(out=out_rows[:, :, c * CHUNK : (c + 1) * CHUNK], in_=res[:])
+
+        weigh_candidates(0)
+        for c in range(1, CHUNKS):
+            weigh_candidates(c)
+            read_out(c - 1)
+        last = CHUNKS - 1
+        words, scales = quantise(z2_bf[last], "y%d" % last)
+        for half in range(2):
+            bank = product(w2_words, w2_scales, words[:], scales[:], first=2 * half, count=2)
+            res = keep.tile([P, 2, CHUNK], F32, name="res_last%d" % half)
+            if half == 0:
+                nc.scalar.copy(out=res[:], in_=bank[:])
+            else:
+                nc.vector.tensor_copy(out=res[:], in_=bank[:])
+            nc.sync.dma_start(out=out_rows[:, 2 * half : 2 * half + 2, last * CHUNK :], in_=res[:])

@@ -13,6 +13,7 @@ U16 = mybir.dt.uint16
 U8 = mybir.dt.uint8
 FP8X4 = mybir.dt.float8_e4m3fn_x4
 MULT = mybir.AluOpType.mult
+COPY = mybir.ActivationFunctionType.Copy
 SIGMOID = mybir.ActivationFunctionType.Sigmoid
 
 P = 128
@@ -28,6 +29,7 @@ def tile_picked_candread_sigmoid_p_kernel(
     nc = tc.nc
     with ExitStack() as ctx:
         keep = ctx.enter_context(tc.tile_pool(name="keep", bufs=1))
+        shared = ctx.enter_context(tc.tile_pool(name="shared", bufs=1))
         psum = ctx.enter_context(tc.psum_pool(name="psum", bufs=8))
 
         offs_sb = keep.tile([P, S // 16], U16, name="offs_sb")
@@ -48,11 +50,14 @@ def tile_picked_candread_sigmoid_p_kernel(
         nc.scalar.activation(warm[:, 1:2], warm[:, 0:1], SIGMOID)
 
         w1_raw = [keep.tile([P, PACK, HALF], F32, name="w1_raw%d" % i) for i in range(2)]
-        w2_raw = [keep.tile([P, PACK, HALF], F32, name="w2_raw%d" % i) for i in range(2)]
+        w2_raw = [
+            shared.tile([P, PACK, HALF], F32, name="w2_raw0", align_bytes=64, offset=0),
+            keep.tile([P, PACK, HALF], F32, name="w2_raw1"),
+        ]
         w1_rows = w1.rearrange("(p j) c -> p j c", j=PACK)
         w2_rows = w2.rearrange("(p j) c -> p j c", j=PACK)
-        nc.sync.dma_start(out=w1_raw[0][:], in_=w1_rows[:, :, 0:HALF])
         nc.sync.dma_start(offs_sb[:], offs)
+        nc.sync.dma_start(out=w1_raw[0][:], in_=w1_rows[:, :, 0:HALF])
         nc.sync.dma_start(cand_sb[:], cand)
         nc.sync.dma_start(out=w1_raw[1][:], in_=w1_rows[:, :, HALF:])
         nc.sync.dma_start(
@@ -62,7 +67,7 @@ def tile_picked_candread_sigmoid_p_kernel(
         for i in range(2):
             nc.sync.dma_start(out=w2_raw[i][:], in_=w2_rows[:, :, i * HALF : (i + 1) * HALF])
         nc.gpsimd.dma_start(out=gs_sb[:], in_=gs.rearrange("(p t) o -> p (t o)", t=PACK))
-        nc.gpsimd.dma_start(out=gt_sb[:], in_=gt.rearrange("(p t) o -> p (t o)", t=PACK))
+        nc.sync.dma_start(out=gt_sb[:], in_=gt.rearrange("(p t) o -> p (t o)", t=PACK))
 
         tok_scales = keep.tile([P, S], U8, name="tok_scales", align_bytes=64)
         cand_scales_listed = keep.tile([P, V], U8, name="cand_scales_listed", align_bytes=64)
@@ -97,7 +102,8 @@ def tile_picked_candread_sigmoid_p_kernel(
         )
 
         w2_bf = keep.tile([P, N, PACK], BF16, name="w2_bf", align_bytes=64)
-        for i in range(2):
+
+        def interleave_w2(i):
             nc.scalar.copy(
                 out=w2_bf[:, HALF * i : HALF * (i + 1), :].rearrange("p (c e) j -> p c j e", e=4),
                 in_=w2_raw[i][:].rearrange("p j (c e) -> p c j e", e=4),
@@ -125,14 +131,17 @@ def tile_picked_candread_sigmoid_p_kernel(
             )
             return words, scales
 
-        h_banks = []
-        for c in range(CHUNKS):
+        h_banks = {}
+        for c in (0, 1, 3, 2):
             lo = (c % 2) * CHUNK
-            h_banks.append(
-                product(w1_words, w1_scales, tok_words[c // 2][:, lo : lo + CHUNK], tok_scales[:, c * CHUNK : (c + 1) * CHUNK])
+            h_banks[c] = product(
+                w1_words, w1_scales, tok_words[c // 2][:, lo : lo + CHUNK], tok_scales[:, c * CHUNK : (c + 1) * CHUNK]
             )
 
-        z_bf = [keep.tile([P, CHUNK, PACK], BF16, name="z_bf%d" % c, align_bytes=64) for c in range(CHUNKS)]
+        z_bf = {
+            c: shared.tile([P, CHUNK, PACK], BF16, name="z_bf%d" % c, align_bytes=64, offset=1024 * c) for c in (0, 2, 3)
+        }
+        z_bf[1] = keep.tile([P, CHUNK, PACK], BF16, name="z_bf1", align_bytes=64)
         sig = [keep.tile([P, CHUNK, PACK], F32, name="sig%d" % c) for c in range(CHUNKS)]
         z2_bf = [keep.tile([P, CHUNK, PACK], BF16, name="z2_bf%d" % c, align_bytes=64) for c in range(CHUNKS)]
         gs_wide = gs_sb[:].unsqueeze(1).to_broadcast([P, CHUNK, PACK])
@@ -146,10 +155,22 @@ def tile_picked_candread_sigmoid_p_kernel(
             bank = product(cand_words, cand_scales, words[:], scales[:])
             nc.scalar.activation(sig[c][:], bank[:].rearrange("p t n -> p n t"), SIGMOID, scale=0.0625)
 
+        interleave_w2(0)
+        z_pairs = shared.tile([P, 2, CHUNK, 2], BF16, name="z_pairs", align_bytes=64, offset=1024)
+        for t in range(PACK):
+            nc.scalar.activation(z_pairs[:, t // 2, :, t % 2], h_banks[1][:, t, :], COPY, scale=gs_sb[:, t : t + 1])
+        interleave_w2(1)
         weigh_features(0)
-        for c in range(1, CHUNKS):
-            weigh_features(c)
-            score(c - 1)
+        weigh_features(3)
+        score(0)
+        weigh_features(2)
+        score(3)
+        nc.vector.tensor_copy(
+            out=z_bf[1][:].rearrange("p n t -> p (n t)").bitcast(I32).rearrange("p (n u) -> p n u", u=2),
+            in_=z_pairs[:].rearrange("p u n e -> p (u n e)").bitcast(I32).rearrange("p (u n) -> p n u", u=2),
+        )
+        score(2)
+        score(1)
         w2_words = keep.tile([P, N], U32, name="w2_words", align_bytes=64)
         w2_scales = keep.tile([P, N], U8, name="w2_scales", align_bytes=64)
         nc.vector.quantize_mx(
@@ -157,7 +178,6 @@ def tile_picked_candread_sigmoid_p_kernel(
             scales=w2_scales[:],
             in_=w2_bf[:].rearrange("p m j -> p (m j)"),
         )
-        score(CHUNKS - 1)
 
         out_rows = out.rearrange("(b p) n -> p b n", p=P)
 
@@ -171,17 +191,28 @@ def tile_picked_candread_sigmoid_p_kernel(
             nc.scalar.copy(out=res[:], in_=bank[:])
             nc.sync.dma_start(out=out_rows[:, :, c * CHUNK : (c + 1) * CHUNK], in_=res[:])
 
+        res_late = [keep.tile([P, 2, 2 * CHUNK], F32, name="res_late%d" % half) for half in range(2)]
+
+        def read_out_late(c):
+            words, scales = quantise(z2_bf[c], "y%d" % c)
+            cols = slice((c - 1) * CHUNK, c * CHUNK)
+            for half in range(2):
+                bank = product(w2_words, w2_scales, words[:], scales[:], first=2 * half, count=2)
+                if half == 0:
+                    nc.scalar.copy(out=res_late[half][:, :, cols], in_=bank[:])
+                else:
+                    late_banks.append((cols, bank))
+
+        late_banks = []
         weigh_candidates(0)
-        for c in range(1, CHUNKS):
-            weigh_candidates(c)
-            read_out(c - 1)
-        last = CHUNKS - 1
-        words, scales = quantise(z2_bf[last], "y%d" % last)
+        weigh_candidates(3)
+        read_out(0)
+        weigh_candidates(2)
+        read_out(3)
+        weigh_candidates(1)
+        read_out_late(2)
+        read_out_late(1)
+        for cols, bank in late_banks:
+            nc.vector.tensor_copy(out=res_late[1][:, :, cols], in_=bank[:])
         for half in range(2):
-            bank = product(w2_words, w2_scales, words[:], scales[:], first=2 * half, count=2)
-            res = keep.tile([P, 2, CHUNK], F32, name="res_last%d" % half)
-            if half == 0:
-                nc.scalar.copy(out=res[:], in_=bank[:])
-            else:
-                nc.vector.tensor_copy(out=res[:], in_=bank[:])
-            nc.sync.dma_start(out=out_rows[:, 2 * half : 2 * half + 2, last * CHUNK :], in_=res[:])
+            nc.sync.dma_start(out=out_rows[:, 2 * half : 2 * half + 2, CHUNK : 3 * CHUNK], in_=res_late[half][:])

from contextlib import ExitStack

import concourse.mybir as mybir

K, T, S, V, N, H = 512, 2048, 512, 512, 512, 512
FLOPS = 2 * K * H * S + 2 * K * V * S + 2 * V * N * S

F32 = mybir.dt.float32
BF16 = mybir.dt.bfloat16
I32 = mybir.dt.int32
U32 = mybir.dt.uint32
U16 = mybir.dt.uint16
U8 = mybir.dt.uint8
FP8X4 = mybir.dt.float8_e4m3fn_x4
MULT = mybir.AluOpType.mult
COPY = mybir.ActivationFunctionType.Copy
SIGMOID = mybir.ActivationFunctionType.Sigmoid

P = 128
PACK = 4
CHUNK = 128
CHUNKS = S // CHUNK
HALF = 256


def tile_picked_candread_sigmoid_p_kernel(
    tc, x_words, x_scales, w1, gs, gt, w2, offs, cand, out
):
    nc = tc.nc
    with ExitStack() as ctx:
        keep = ctx.enter_context(tc.tile_pool(name="keep", bufs=1))
        shared = ctx.enter_context(tc.tile_pool(name="shared", bufs=1))
        psum = ctx.enter_context(tc.psum_pool(name="psum", bufs=8))

        offs_sb = keep.tile([P, S // 16], U16, name="offs_sb")
        cand_sb = keep.tile([P, V // 16], U16, name="cand_sb")
        table_words = keep.tile([P, T], U32, name="table_words", align_bytes=64)
        table_scales = keep.tile([P, T], U8, name="table_scales", align_bytes=64)
        gs_sb = keep.tile([P, PACK], F32, name="gs_sb")
        gt_sb = keep.tile([P, PACK], F32, name="gt_sb")
        warm = keep.tile([P, 2], F32, name="warm")

        nc.vector.memset(table_scales[:].bitcast(I32), 0)
        for q in range(4):
            nc.scalar.dma_start(
                out=table_scales[32 * q : 32 * q + 4, :].bitcast(I32),
                in_=x_scales[0, 4 * q : 4 * q + 4, :].bitcast(I32),
            )
        nc.vector.memset(warm[:, 0:1], 0.0)
        nc.scalar.activation(warm[:, 1:2], warm[:, 0:1], SIGMOID)

        w1_raw = [keep.tile([P, PACK, HALF], F32, name="w1_raw%d" % i) for i in range(2)]
        w2_raw = [
            shared.tile([P, PACK, HALF], F32, name="w2_raw0", align_bytes=64, offset=0),
            keep.tile([P, PACK, HALF], F32, name="w2_raw1"),
        ]
        w1_rows = w1.rearrange("(p j) c -> p j c", j=PACK)
        w2_rows = w2.rearrange("(p j) c -> p j c", j=PACK)
        nc.sync.dma_start(offs_sb[:], offs)
        nc.sync.dma_start(out=w1_raw[0][:], in_=w1_rows[:, :, 0:HALF])
        nc.sync.dma_start(cand_sb[:], cand)
        nc.sync.dma_start(out=w1_raw[1][:], in_=w1_rows[:, :, HALF:])
        nc.sync.dma_start(
            out=table_words[:].bitcast(I32),
            in_=x_words[0].rearrange("p n t -> p (n t)").bitcast(I32),
        )
        for i in range(2):
            nc.sync.dma_start(out=w2_raw[i][:], in_=w2_rows[:, :, i * HALF : (i + 1) * HALF])
        nc.gpsimd.dma_start(out=gs_sb[:], in_=gs.rearrange("(p t) o -> p (t o)", t=PACK))
        nc.sync.dma_start(out=gt_sb[:], in_=gt.rearrange("(p t) o -> p (t o)", t=PACK))

        tok_scales = keep.tile([P, S], U8, name="tok_scales", align_bytes=64)
        cand_scales_listed = keep.tile([P, V], U8, name="cand_scales_listed", align_bytes=64)
        cand_scales = keep.tile([P, V], U8, name="cand_scales", align_bytes=64)
        nc.vector.tensor_copy(tok_scales[:], table_scales[:].indirect(offs_sb[:]))
        nc.vector.tensor_copy(cand_scales_listed[:], table_scales[:].indirect(cand_sb[:]))
        nc.vector.tensor_copy(
            out=cand_scales[:].rearrange("p (t m) -> p m t", t=PACK),
            in_=cand_scales_listed[:].rearrange("p (m t) -> p m t", t=PACK),
        )

        w1_bf = keep.tile([P, PACK, P, PACK], BF16, name="w1_bf", align_bytes=64)
        for i in range(2):
            nc.scalar.copy(
                out=w1_bf[:, :, 64 * i : 64 * (i + 1), :].rearrange("p t m j -> p m j t"),
                in_=w1_raw[i][:].rearrange("p j (m t) -> p m j t", t=PACK),
            )
        w1_words = keep.tile([P, H], U32, name="w1_words", align_bytes=64)
        w1_scales = keep.tile([P, H], U8, name="w1_scales", align_bytes=64)
        nc.vector.quantize_mx(
            out=w1_words[:].bitcast(FP8X4),
            scales=w1_scales[:],
            in_=w1_bf[:].rearrange("p t m j -> p (t m j)"),
        )

        tok_words = [keep.tile([P, HALF], U32, name="tok_words%d" % i, align_bytes=64) for i in range(2)]
        for i in range(2):
            nc.vector.tensor_copy(tok_words[i][:], table_words[:].indirect(offs_sb[:, 16 * i : 16 * (i + 1)]))
        cand_words = keep.tile([P, V], U32, name="cand_words", align_bytes=64)
        nc.vector.tensor_copy(
            cand_words[:].rearrange("p (t m) -> p m t", t=PACK), table_words[:].indirect(cand_sb[:])
        )

        w2_bf = keep.tile([P, N, PACK], BF16, name="w2_bf", align_bytes=64)

        def interleave_w2(i):
            nc.scalar.copy(
                out=w2_bf[:, HALF * i : HALF * (i + 1), :].rearrange("p (c e) j -> p c j e", e=4),
                in_=w2_raw[i][:].rearrange("p j (c e) -> p c j e", e=4),
            )

        def product(words, scales, rhs_words, rhs_scales, first=0, count=PACK):
            bank = psum.tile([P, count, CHUNK], F32, name="bank")
            for t in range(first, first + count):
                nc.tensor.matmul_mx(
                    out=bank[:, t - first, :],
                    lhsT=words[:, P * t : P * (t + 1)].bitcast(FP8X4),
                    lhsT_scale=scales[:, P * t : P * (t + 1)],
                    rhs=rhs_words.bitcast(FP8X4),
                    rhs_scale=rhs_scales,
                    start=True,
                    stop=True,
                )
            return bank

        def quantise(values, name):
            words = keep.tile([P, CHUNK], U32, name=name + "_words", align_bytes=64)
            scales = keep.tile([P, CHUNK], U8, name=name + "_scales", align_bytes=64)
            nc.vector.quantize_mx(
                out=words[:].bitcast(FP8X4), scales=scales[:], in_=values[:].rearrange("p n t -> p (n t)")
            )
            return words, scales

        h_banks = {}
        for c in (0, 1, 3, 2):
            lo = (c % 2) * CHUNK
            h_banks[c] = product(
                w1_words, w1_scales, tok_words[c // 2][:, lo : lo + CHUNK], tok_scales[:, c * CHUNK : (c + 1) * CHUNK]
            )

        z_bf = {
            c: shared.tile([P, CHUNK, PACK], BF16, name="z_bf%d" % c, align_bytes=64, offset=1024 * c) for c in (0, 2, 3)
        }
        z_bf[1] = keep.tile([P, CHUNK, PACK], BF16, name="z_bf1", align_bytes=64)
        sig = [keep.tile([P, CHUNK, PACK], F32, name="sig%d" % c) for c in range(CHUNKS)]
        z2_bf = [keep.tile([P, CHUNK, PACK], BF16, name="z2_bf%d" % c, align_bytes=64) for c in range(CHUNKS)]
        gs_wide = gs_sb[:].unsqueeze(1).to_broadcast([P, CHUNK, PACK])
        gt_wide = gt_sb[:].unsqueeze(1).to_broadcast([P, CHUNK, PACK])

        def weigh_features(c):
            nc.vector.tensor_tensor(z_bf[c][:], h_banks[c][:].rearrange("p t n -> p n t"), gs_wide, MULT)

        def score(c):
            words, scales = quantise(z_bf[c], "z%d" % c)
            bank = product(cand_words, cand_scales, words[:], scales[:])
            nc.scalar.activation(sig[c][:], bank[:].rearrange("p t n -> p n t"), SIGMOID, scale=0.0625)

        interleave_w2(0)
        z_pairs = shared.tile([P, 2, CHUNK, 2], BF16, name="z_pairs", align_bytes=64, offset=1024)
        for t in range(PACK):
            nc.scalar.activation(z_pairs[:, t // 2, :, t % 2], h_banks[1][:, t, :], COPY, scale=gs_sb[:, t : t + 1])
        interleave_w2(1)
        weigh_features(0)
        weigh_features(3)
        score(0)
        weigh_features(2)
        score(3)
        nc.vector.tensor_copy(
            out=z_bf[1][:].rearrange("p n t -> p (n t)").bitcast(I32).rearrange("p (n u) -> p n u", u=2),
            in_=z_pairs[:].rearrange("p u n e -> p (u n e)").bitcast(I32).rearrange("p (u n) -> p n u", u=2),
        )
        score(2)
        score(1)
        w2_words = keep.tile([P, N], U32, name="w2_words", align_bytes=64)
        w2_scales = keep.tile([P, N], U8, name="w2_scales", align_bytes=64)
        nc.vector.quantize_mx(
            out=w2_words[:].bitcast(FP8X4),
            scales=w2_scales[:],
            in_=w2_bf[:].rearrange("p m j -> p (m j)"),
        )

        out_rows = out.rearrange("(b p) n -> p b n", p=P)

        def weigh_candidates(c):
            nc.vector.tensor_tensor(z2_bf[c][:], sig[c][:], gt_wide, MULT)

        def read_out(c):
            words, scales = quantise(z2_bf[c], "y%d" % c)
            bank = product(w2_words, w2_scales, words[:], scales[:])
            res = keep.tile([P, PACK, CHUNK], F32, name="res%d" % c)
            nc.scalar.copy(out=res[:], in_=bank[:])
            nc.sync.dma_start(out=out_rows[:, :, c * CHUNK : (c + 1) * CHUNK], in_=res[:])

        res_late = [keep.tile([P, 2, 2 * CHUNK], F32, name="res_late%d" % half) for half in range(2)]

        def read_out_late(c):
            words, scales = quantise(z2_bf[c], "y%d" % c)
            cols = slice((c - 1) * CHUNK, c * CHUNK)
            for half in range(2):
                bank = product(w2_words, w2_scales, words[:], scales[:], first=2 * half, count=2)
                if half == 0:
                    nc.scalar.copy(out=res_late[half][:, :, cols], in_=bank[:])
                else:
                    late_banks.append((cols, bank))

        late_banks = []
        weigh_candidates(0)
        weigh_candidates(3)
        read_out(0)
        weigh_candidates(2)
        read_out(3)
        weigh_candidates(1)
        read_out_late(2)
        read_out_late(1)
        for cols, bank in late_banks:
            nc.vector.tensor_copy(out=res_late[1][:, :, cols], in_=bank[:])
        for half in range(2):
            nc.sync.dma_start(out=out_rows[:, 2 * half : 2 * half + 2, CHUNK : 3 * CHUNK], in_=res_late[half][:])
